import numpy as np
import ml_dtypes


def mxq(x, axis, fmt="e4m3"):
    dtype, down = {"e4m3": (ml_dtypes.float8_e4m3fn, 7), "e5m2": (ml_dtypes.float8_e5m2, 14)}[fmt]
    v = np.moveaxis(np.asarray(x, np.float32).astype(ml_dtypes.bfloat16).astype(np.float64), axis, -1)
    blocks = v.reshape(v.shape[:-1] + (-1, 32))
    amax = np.abs(blocks).max(-1, keepdims=True)
    byte = np.maximum(np.where(amax > 0, np.frexp(amax)[1] - 1 + 127, 0) - down, 1)
    scale = np.exp2(byte - 127.0)
    codes = (blocks / scale).astype(np.float32).astype(dtype).astype(np.float64)
    return np.moveaxis((codes * scale).reshape(v.shape), -1, axis)


WIDE = False


def mx_kscale(k):
    if not WIDE:
        return np.ones(k)
    levels = np.array([30, -30])
    if k % 512:
        return np.exp2(np.random.permutation(np.resize(levels, k // 32))).repeat(32)
    a = np.empty((k // 512, 16))
    for p in range(k // 512):
        a[p, :8] = np.random.permutation(np.resize(levels, 8))
        for g in range(8):
            far = levels[np.abs(levels - a[p, g]) >= 10]
            a[p, g + 8] = far[np.random.randint(len(far))]
    return np.exp2(a.ravel()).repeat(32)


def f64(x):
    return np.asarray(x).astype(np.float64)


def striped(idx):
    return np.tile(idx.reshape(-1, 16).T, (8, 1)).astype(np.uint16)


def unstriped(offs):
    return offs[:16].T.reshape(-1).astype(np.int64)


def split(x):
    m, e = np.frexp(f64(x))
    hi = np.ldexp(np.trunc(16.0 * m) / 16.0, e)
    return hi, f64(x) - hi


K, N, T, J = 512, 1024, 2048, 1024


def setup_inputs():
    n = np.random.standard_normal
    s = mx_kscale(K)[:, None]
    m = np.exp(0.5 * n((1, J)))
    return {
        "dy": (m * n((K, J)) * s).astype(np.float32),
        "w": (n((K, N)) / np.sqrt(K) / s).astype(np.float32),
        "d": (0.5 + 0.3 * n((N, J))).astype(np.float32),
        "wgo": np.tile(np.random.uniform(0.5, 2.0, J), (128, 1)).astype(np.float32),
        "offs": striped(np.random.permutation(T)[:J]),
    }


def reference(dy, w, d, wgo, offs):
    idx = unstriped(offs)
    dy_ = mxq(f64(dy), 0, "e5m2")
    w_hi, w_lo = split(w)
    w_hi_, w_lo_ = mxq(w_hi, 0, "e4m3"), mxq(w_lo, 0, "e4m3")
    dx = w_hi_.T @ dy_ + w_lo_.T @ dy_
    out = np.zeros((N, T))
    out[:, idx] = f64(wgo)[0] * (dx * f64(d))
    return out

@@ -1,0 +1,264 @@
+from contextlib import ExitStack
+
+import concourse.mybir as mybir
+from concourse.masks import make_identity
+
+K, N, T, J = 512, 1024, 2048, 1024
+FLOPS = 2 * 2 * K * N * J
+
+F32 = mybir.dt.float32
+BF16 = mybir.dt.bfloat16
+I32 = mybir.dt.int32
+U32 = mybir.dt.uint32
+U16 = mybir.dt.uint16
+U8 = mybir.dt.uint8
+E4M3 = mybir.dt.float8_e4m3fn_x4
+E5M2 = mybir.dt.float8_e5m2_x4
+ALU = mybir.AluOpType
+COPY = mybir.ActivationFunctionType.Copy
+
+P = 128
+PACK = 4
+HALF = 512
+NB = N // P
+HI_MASK = -983056
+COPY_SCATTER = (4, 5, 6, 7)
+N_WIN = 3
+
+
+def tile_list_embg_hl_mul_kernel(tc, dy, w, d, wgo, offs, out):
+    nc = tc.nc
+    with ExitStack() as ctx:
+        lists = ctx.enter_context(tc.tile_pool(name="lists", bufs=1))
+        keep = ctx.enter_context(tc.tile_pool(name="keep", bufs=1))
+        ring = ctx.enter_context(tc.tile_pool(name="ring", bufs=3))
+        mm_ps = ctx.enter_context(tc.psum_pool(name="mm_ps", bufs=4))
+        t1_ps = ctx.enter_context(tc.psum_pool(name="t1_ps", bufs=2))
+        t2_ps = ctx.enter_context(tc.psum_pool(name="t2_ps", bufs=2))
+
+        offsets = lists.tile([P, J // 16], U16, name="offsets")
+        nc.sync.dma_start(offsets[:], offs)
+
+        w4 = w.rearrange("(p t) n -> p t n", t=PACK)
+        dy4 = dy.rearrange("(p t) j -> p t j", t=PACK)
+
+        def load(name, shape, src):
+            tl = keep.tile(shape, F32, name=name)
+            nc.sync.dma_start(out=tl[:], in_=src)
+            return tl
+
+        ident = keep.tile([P, P], F32, name="ident")
+        make_identity(nc, ident[:])
+        stage = keep.tile([P, P], F32, name="stage")
+        nc.scalar.activation(out=stage[:], in_=ident[:], func=COPY)
+        nc.scalar.dma_start(out=stage[0:8, :], in_=wgo[0, :].rearrange("(c p) -> c p", p=P))
+
+        windows = []
+        for i in range(N_WIN):
+            win = keep.tile([P, T], F32, name=f"win{i}")
+            nc.vector.memset(win[:], 0.0)
+            windows.append(win)
+
+        w_raw = {}
+        dy_raw = {}
+        d_raw = {}
+        w_raw[0] = load("w0", [P, PACK, P], w4[:, :, 0:P])
+        dy_raw[0] = load("dy0", [P, PACK, 256], dy4[:, :, 0:256])
+        dy_raw[1] = load("dy1", [P, PACK, 256], dy4[:, :, 256:512])
+        w_raw[1] = load("w1", [P, PACK, P], w4[:, :, P : 2 * P])
+        d_raw[0, 0] = load("d00", [P, HALF], d[0:P, 0:HALF])
+        wgo_a = load("wgo_a", [P, HALF], wgo[:, 0:HALF])
+        d_raw[1, 0] = load("d10", [P, HALF], d[P : 2 * P, 0:HALF])
+        dy_raw[2] = load("dy2", [P, PACK, 256], dy4[:, :, 512:768])
+        dy_raw[3] = load("dy3", [P, PACK, 256], dy4[:, :, 768:1024])
+        d_raw[0, 1] = load("d01", [P, HALF], d[0:P, HALF:J])
+        d_raw[1, 1] = load("d11", [P, HALF], d[P : 2 * P, HALF:J])
+        for b in range(2, NB):
+            if b % 2 == 0:
+                pair = load(f"w{b}", [P, PACK, 2 * P], w4[:, :, b * P : (b + 2) * P])
+                w_raw[b] = pair[:, :, 0:P]
+                w_raw[b + 1] = pair[:, :, P : 2 * P]
+            whole = load(f"d{b}", [P, J], d[b * P : (b + 1) * P, :])
+            d_raw[b, 0] = whole[:, 0:HALF]
+            d_raw[b, 1] = whole[:, HALF:J]
+
+        wgo_ps = t1_ps.tile([P, HALF], F32, name="t1")
+        nc.tensor.transpose(wgo_ps[:, 0:P], stage[:], ident[:])
+        wgo_t = keep.tile([P, 8], F32, name="wgo_t")
+        nc.scalar.copy(out=wgo_t[:], in_=wgo_ps[:, 0:8])
+
+        dy_codes = keep.tile([P, J], U32, name="dy_codes", align_bytes=64)
+        dy_scales = keep.tile([P, J], U8, name="dy_scales", align_bytes=64)
+
+        def il(ap):
+            return ap.rearrange("p (c i t) -> p c t i", i=4, t=PACK)
+
+        def pl(ap):
+            return ap.rearrange("p t (c i) -> p c t i", i=4)
+
+        dy_bf = {}
+
+        def cast_dy(q, vec_cols):
+            tl = keep.tile([P, 256 * PACK], BF16, name=f"dybf{q}", align_bytes=64)
+            dy_bf[q] = tl
+            s = 256 - vec_cols
+            nc.scalar.copy(out=il(tl[:, 0 : s * PACK]), in_=pl(dy_raw[q][:, :, 0:s]))
+            if vec_cols:
+                nc.vector.tensor_copy(out=il(tl[:, s * PACK :]), in_=pl(dy_raw[q][:, :, s:256]))
+
+        def quant_dy(q):
+            cols = slice(q * 256, (q + 1) * 256)
+            nc.vector.quantize_mx(out=dy_codes[:, cols].bitcast(E5M2), scales=dy_scales[:, cols], in_=dy_bf[q][:])
+
+        top = {}
+        hl = {}
+        w_codes = {}
+        w_scales = {}
+
+        def top_w(b, eng):
+            tl = ring.tile([P, P * PACK], BF16, name="top", align_bytes=64)
+            top[b] = tl
+            src = pl(w_raw[b][:, :, :].bitcast(BF16)[:, :, 1::2])
+            if eng == "v":
+                nc.vector.tensor_copy(out=il(tl[:]), in_=src)
+            else:
+                nc.scalar.copy(out=il(tl[:]), in_=src)
+
+        def hi_w(b):
+            tl = ring.tile([P, 2 * P * PACK], BF16, name="hl", align_bytes=64)
+            hl[b] = tl
+            nc.vector.tensor_scalar(
+                out=tl[:, 0 : P * PACK].bitcast(I32), in0=top[b][:].bitcast(I32),
+                scalar1=HI_MASK, scalar2=None, op0=ALU.bitwise_and,
+            )
+
+        def lo_w(b):
+            tl = hl[b]
+            nc.vector.tensor_tensor(
+                out=il(tl[:, P * PACK :]), in0=pl(w_raw[b][:, :, :]), in1=il(tl[:, 0 : P * PACK]), op=ALU.subtract
+            )
+
+        def quant_w(b):
+            w_codes[b] = keep.tile([P, 2 * P], U32, name=f"wc{b}", align_bytes=64)
+            w_scales[b] = keep.tile([P, 2 * P], U8, name=f"ws{b}", align_bytes=64)
+            nc.vector.quantize_mx(out=w_codes[b][:].bitcast(E4M3), scales=w_scales[b][:], in_=hl[b][:])
+
+        acc = {}
+
+        def matmul(b, h):
+            ps = mm_ps.tile([P, HALF], F32, name="mm")
+            acc[b, h] = ps
+            cols = slice(h * HALF, (h + 1) * HALF)
+            for part in range(2):
+                wc = slice(part * P, (part + 1) * P)
+                nc.tensor.matmul_mx(
+                    out=ps[:], lhsT=w_codes[b][:, wc].bitcast(E4M3), lhsT_scale=w_scales[b][:, wc],
+                    rhs=dy_codes[:, cols].bitcast(E5M2), rhs_scale=dy_scales[:, cols],
+                    start=(part == 0), stop=(part == 1),
+                )
+
+        dx = {}
+        dw = {}
+
+        def blk(store, b, name):
+            if b not in store:
+                store[b] = ring.tile([P, J], F32, name=name)
+            return store[b]
+
+        def weigh_d(b, h):
+            t1 = t1_ps.tile([P, HALF], F32, name="t1")
+            for c in range(4):
+                nc.tensor.transpose(t1[:, c * P : (c + 1) * P], d_raw[b, h][:, c * P : (c + 1) * P], ident[:])
+            dt = ring.tile([P, HALF], F32, name="dt")
+            for c in range(4):
+                nc.scalar.activation(
+                    out=dt[:, c * P : (c + 1) * P], in_=t1[:, c * P : (c + 1) * P], func=COPY,
+                    scale=wgo_t[:, 4 * h + c : 4 * h + c + 1],
+                )
+            t2 = t2_ps.tile([P, HALF], F32, name="t2")
+            for c in range(4):
+                nc.tensor.transpose(t2[:, c * P : (c + 1) * P], dt[:, c * P : (c + 1) * P], ident[:])
+            nc.scalar.copy(out=blk(dw, b, "dw")[:, h * HALF : (h + 1) * HALF], in_=t2[:])
+
+        def copy_dx(b, h):
+            nc.scalar.copy(out=blk(dx, b, "dx")[:, h * HALF : (h + 1) * HALF], in_=acc[b, h][:])
+
+        def scatter_half(b, h, other):
+            cols = slice(h * HALF, (h + 1) * HALF)
+            nc.vector.tensor_tensor(
+                out=windows[b % N_WIN][:].indirect(offsets[:, h * 32 : (h + 1) * 32]),
+                in0=dx[b][:, cols], in1=other, op=ALU.mult,
+            )
+
+        def store(b):
+            nc.sync.dma_start(out=out[b * P : (b + 1) * P, :], in_=windows[b % N_WIN][:])
+
+        top_w(0, "v")
+        hi_w(0)
+        lo_w(0)
+        cast_dy(0, 0)
+        quant_w(0)
+        quant_dy(0)
+        cast_dy(1, 128)
+        quant_dy(1)
+        top_w(1, "s")
+        matmul(0, 0)
+        hi_w(1)
+        lo_w(1)
+        nc.vector.tensor_tensor(out=blk(dx, 0, "dx")[:, 0:HALF], in0=acc[0, 0][:], in1=d_raw[0, 0][:], op=ALU.mult)
+        quant_w(1)
+        weigh_d(1, 0)
+        matmul(1, 0)
+        copy_dx(1, 0)
+        scatter_half(0, 0, wgo_a[:])
+        cast_dy(2, 0)
+        cast_dy(3, 0)
+        quant_dy(2)
+        quant_dy(3)
+        weigh_d(0, 1)
+        matmul(0, 1)
+        copy_dx(0, 1)
+        scatter_half(1, 0, dw[1][:, 0:HALF])
+        top_w(2, "s")
+        weigh_d(1, 1)
+        matmul(1, 1)
+        copy_dx(1, 1)
+        hi_w(2)
+        scatter_half(0, 1, dw[0][:, HALF:J])
+        store(0)
+
+        def prepare(b):
+            for h in range(2):
+                weigh_d(b, h)
+                matmul(b, h)
+                if b not in COPY_SCATTER:
+                    copy_dx(b, h)
+
+        lo_w(2)
+        top_w(3, "s")
+        hi_w(3)
+        quant_w(2)
+        prepare(2)
+        scatter_half(1, 1, dw[1][:, HALF:J])
+        store(1)
+
+        for b in range(2, NB):
+            if b + 1 < NB:
+                lo_w(b + 1)
+                if b + 2 < NB:
+                    top_w(b + 2, "s")
+                    hi_w(b + 2)
+                quant_w(b + 1)
+            win = windows[b % N_WIN][:].indirect(offsets[:])
+            if b in COPY_SCATTER:
+                for h in range(2):
+                    cols = slice(h * HALF, (h + 1) * HALF)
+                    nc.vector.tensor_tensor(out=blk(dx, b, "dx")[:, cols], in0=acc[b, h][:], in1=dw[b][:, cols], op=ALU.mult)
+                if b + 1 < NB:
+                    prepare(b + 1)
+                nc.vector.tensor_copy(out=win, in_=dx[b][:])
+            else:
+                if b + 1 < NB:
+                    prepare(b + 1)
+                nc.vector.tensor_tensor(out=win, in0=dx[b][:], in1=dw[b][:], op=ALU.mult)
+            store(b)

@@ -22,7 +22,6 @@ PACK = 4
 HALF = 512
 NB = N // P
 HI_MASK = -983056
-COPY_SCATTER = (4, 5, 6, 7)
 N_WIN = 3
 
 
@@ -31,7 +30,7 @@ def tile_list_embg_hl_mul_kernel(tc, dy, w, d, wgo, offs, out):
     with ExitStack() as ctx:
         lists = ctx.enter_context(tc.tile_pool(name="lists", bufs=1))
         keep = ctx.enter_context(tc.tile_pool(name="keep", bufs=1))
-        ring = ctx.enter_context(tc.tile_pool(name="ring", bufs=3))
+        ring = ctx.enter_context(tc.tile_pool(name="ring", bufs=4))
         mm_ps = ctx.enter_context(tc.psum_pool(name="mm_ps", bufs=4))
         t1_ps = ctx.enter_context(tc.psum_pool(name="t1_ps", bufs=2))
         t2_ps = ctx.enter_context(tc.psum_pool(name="t2_ps", bufs=2))
@@ -43,66 +42,80 @@ def tile_list_embg_hl_mul_kernel(tc, dy, w, d, wgo, offs, out):
         dy4 = dy.rearrange("(p t) j -> p t j", t=PACK)
 
         def load(name, shape, src):
-            tl = keep.tile(shape, F32, name=name)
+            tl = keep.tile(shape, F32, name=name, tag=name, align_bytes=64)
             nc.sync.dma_start(out=tl[:], in_=src)
             return tl
 
+        ident0 = keep.tile([P, P], F32, name="ident0")
+        make_identity(nc, ident0[:])
         ident = keep.tile([P, P], F32, name="ident")
-        make_identity(nc, ident[:])
-        stage = keep.tile([P, P], F32, name="stage")
-        nc.scalar.activation(out=stage[:], in_=ident[:], func=COPY)
-        nc.scalar.dma_start(out=stage[0:8, :], in_=wgo[0, :].rearrange("(c p) -> c p", p=P))
+        nc.scalar.activation(out=ident[:], in_=ident0[:], func=COPY)
 
-        windows = []
-        for i in range(N_WIN):
-            win = keep.tile([P, T], F32, name=f"win{i}")
-            nc.vector.memset(win[:], 0.0)
-            windows.append(win)
+        windows = {}
+        for i in range(2):
+            windows[i] = keep.tile([P, T], F32, name=f"win{i}")
+            nc.vector.memset(windows[i][:], 0.0)
 
-        w_raw = {}
+        def late_window(i, tag):
+            windows[i] = keep.tile([P, T], F32, name=f"win{i}", tag=tag, align_bytes=64)
+            nc.gpsimd.memset(windows[i][:], 0.0)
+
+        w_unit = {}
         dy_raw = {}
         d_raw = {}
-        w_raw[0] = load("w0", [P, PACK, P], w4[:, :, 0:P])
+        def load_w_pair(b):
+            pair = load(f"w{b}", [P, PACK, 2 * P], w4[:, :, b * P : (b + 2) * P])
+            w_unit[b] = pair
+
+        def load_d(b):
+            whole = load(f"d{b}", [P, J], d[b * P : (b + 1) * P, :])
+            d_raw[b, 0] = whole[:, 0:HALF]
+            d_raw[b, 1] = whole[:, HALF:J]
+
+        w_unit[0] = load("w0", [P, PACK, P], w4[:, :, 0:P])
+        w_unit[1] = load("w1", [P, PACK, P], w4[:, :, P : 2 * P])
+        stage = load("stage", [P, P], wgo.rearrange("r (c p) -> (r c) p", p=P)[0:P, :])
         dy_raw[0] = load("dy0", [P, PACK, 256], dy4[:, :, 0:256])
-        dy_raw[1] = load("dy1", [P, PACK, 256], dy4[:, :, 256:512])
-        w_raw[1] = load("w1", [P, PACK, P], w4[:, :, P : 2 * P])
         d_raw[0, 0] = load("d00", [P, HALF], d[0:P, 0:HALF])
-        wgo_a = load("wgo_a", [P, HALF], wgo[:, 0:HALF])
+        dy_raw[1] = load("dy1", [P, PACK, 256], dy4[:, :, 256:512])
+        load_w_pair(2)
+        w_unit[3] = w_unit[2][:, :, P : 2 * P]
+        w_unit[2] = w_unit[2][:, :, 0:P]
         d_raw[1, 0] = load("d10", [P, HALF], d[P : 2 * P, 0:HALF])
         dy_raw[2] = load("dy2", [P, PACK, 256], dy4[:, :, 512:768])
         dy_raw[3] = load("dy3", [P, PACK, 256], dy4[:, :, 768:1024])
         d_raw[0, 1] = load("d01", [P, HALF], d[0:P, HALF:J])
         d_raw[1, 1] = load("d11", [P, HALF], d[P : 2 * P, HALF:J])
-        for b in range(2, NB):
-            if b % 2 == 0:
-                pair = load(f"w{b}", [P, PACK, 2 * P], w4[:, :, b * P : (b + 2) * P])
-                w_raw[b] = pair[:, :, 0:P]
-                w_raw[b + 1] = pair[:, :, P : 2 * P]
-            whole = load(f"d{b}", [P, J], d[b * P : (b + 1) * P, :])
-            d_raw[b, 0] = whole[:, 0:HALF]
-            d_raw[b, 1] = whole[:, HALF:J]
+        load_d(2)
+        load_w_pair(4)
+        load_w_pair(6)
+        for b in range(3, NB):
+            load_d(b)
 
-        wgo_ps = t1_ps.tile([P, HALF], F32, name="t1")
-        nc.tensor.transpose(wgo_ps[:, 0:P], stage[:], ident[:])
         wgo_t = keep.tile([P, 8], F32, name="wgo_t")
-        nc.scalar.copy(out=wgo_t[:], in_=wgo_ps[:, 0:8])
+
+        def turn_wgo():
+            wgo_ps = t1_ps.tile([P, HALF], F32, name="t1")
+            nc.tensor.transpose(wgo_ps[:, 0:P], stage[:], ident[:])
+            nc.scalar.copy(out=wgo_t[:], in_=wgo_ps[:, 0:8])
 
         dy_codes = keep.tile([P, J], U32, name="dy_codes", align_bytes=64)
         dy_scales = keep.tile([P, J], U8, name="dy_scales", align_bytes=64)
 
         def il(ap):
-            return ap.rearrange("p (c i t) -> p c t i", i=4, t=PACK)
+            return ap.rearrange("p (c i t) -> p c t i", i=2, t=PACK)
 
         def pl(ap):
-            return ap.rearrange("p t (c i) -> p c t i", i=4)
+            return ap.rearrange("p t (c i) -> p c t i", i=2)
 
         dy_bf = {}
 
         def cast_dy(q, vec_cols):
-            tl = keep.tile([P, 256 * PACK], BF16, name=f"dybf{q}", align_bytes=64)
+            tl = keep.tile([P, 256 * PACK], BF16, name=f"dybf{q}", tag=f"dybf{q}", align_bytes=64)
             dy_bf[q] = tl
             s = 256 - vec_cols
-            nc.scalar.copy(out=il(tl[:, 0 : s * PACK]), in_=pl(dy_raw[q][:, :, 0:s]))
+            if s:
+                nc.scalar.copy(out=il(tl[:, 0 : s * PACK]), in_=pl(dy_raw[q][:, :, 0:s]))
             if vec_cols:
                 nc.vector.tensor_copy(out=il(tl[:, s * PACK :]), in_=pl(dy_raw[q][:, :, s:256]))
 
@@ -115,33 +128,41 @@ def tile_list_embg_hl_mul_kernel(tc, dy, w, d, wgo, offs, out):
         w_codes = {}
         w_scales = {}
 
-        def top_w(b, eng):
-            tl = ring.tile([P, P * PACK], BF16, name="top", align_bytes=64)
+        def top_w(b, nb, eng):
+            width = nb * P * PACK
+            tl = ring.tile([P, width], BF16, name="top", align_bytes=64)
             top[b] = tl
-            src = pl(w_raw[b][:, :, :].bitcast(BF16)[:, :, 1::2])
+            src = pl(w_unit[b][:, :, :].bitcast(BF16)[:, :, 1::2])
             if eng == "v":
                 nc.vector.tensor_copy(out=il(tl[:]), in_=src)
             else:
                 nc.scalar.copy(out=il(tl[:]), in_=src)
 
-        def hi_w(b):
-            tl = ring.tile([P, 2 * P * PACK], BF16, name="hl", align_bytes=64)
+        def hi_w(b, nb):
+            width = nb * P * PACK
+            tl = keep.tile([P, 2 * width], BF16, name=f"hl{b}", tag=f"hl{b}", align_bytes=64)
             hl[b] = tl
             nc.vector.tensor_scalar(
-                out=tl[:, 0 : P * PACK].bitcast(I32), in0=top[b][:].bitcast(I32),
+                out=tl[:, 0:width].bitcast(I32), in0=top[b][:].bitcast(I32),
                 scalar1=HI_MASK, scalar2=None, op0=ALU.bitwise_and,
             )
 
-        def lo_w(b):
+        def lo_w(b, nb):
+            width = nb * P * PACK
             tl = hl[b]
             nc.vector.tensor_tensor(
-                out=il(tl[:, P * PACK :]), in0=pl(w_raw[b][:, :, :]), in1=il(tl[:, 0 : P * PACK]), op=ALU.subtract
+                out=il(tl[:, width:]), in0=pl(w_unit[b][:, :, :]), in1=il(tl[:, 0:width]), op=ALU.subtract
             )
 
-        def quant_w(b):
-            w_codes[b] = keep.tile([P, 2 * P], U32, name=f"wc{b}", align_bytes=64)
-            w_scales[b] = keep.tile([P, 2 * P], U8, name=f"ws{b}", align_bytes=64)
-            nc.vector.quantize_mx(out=w_codes[b][:].bitcast(E4M3), scales=w_scales[b][:], in_=hl[b][:])
+        def quant_w(b, nb):
+            codes = keep.tile([P, 2 * nb * P], U32, name=f"wc{b}", align_bytes=64)
+            scales = keep.tile([P, 2 * nb * P], U8, name=f"ws{b}", align_bytes=64)
+            nc.vector.quantize_mx(out=codes[:].bitcast(E4M3), scales=scales[:], in_=hl[b][:])
+            for i in range(nb):
+                for part in range(2):
+                    cols = slice((part * nb + i) * P, (part * nb + i + 1) * P)
+                    w_codes[b + i, part] = codes[:, cols]
+                    w_scales[b + i, part] = scales[:, cols]
 
         acc = {}
 
@@ -150,14 +171,13 @@ def tile_list_embg_hl_mul_kernel(tc, dy, w, d, wgo, offs, out):
             acc[b, h] = ps
             cols = slice(h * HALF, (h + 1) * HALF)
             for part in range(2):
-                wc = slice(part * P, (part + 1) * P)
                 nc.tensor.matmul_mx(
-                    out=ps[:], lhsT=w_codes[b][:, wc].bitcast(E4M3), lhsT_scale=w_scales[b][:, wc],
+                    out=ps[:], lhsT=w_codes[b, part].bitcast(E4M3), lhsT_scale=w_scales[b, part],
                     rhs=dy_codes[:, cols].bitcast(E5M2), rhs_scale=dy_scales[:, cols],
                     start=(part == 0), stop=(part == 1),
                 )
 
-        dx = {}
+        dx = {0: keep.tile([P, J], F32, name="dx0", tag="dx0", align_bytes=64)}
         dw = {}
 
         def blk(store, b, name):
@@ -183,82 +203,82 @@ def tile_list_embg_hl_mul_kernel(tc, dy, w, d, wgo, offs, out):
         def copy_dx(b, h):
             nc.scalar.copy(out=blk(dx, b, "dx")[:, h * HALF : (h + 1) * HALF], in_=acc[b, h][:])
 
-        def scatter_half(b, h, other):
-            cols = slice(h * HALF, (h + 1) * HALF)
+        def scatter(b, j0, j1, other):
             nc.vector.tensor_tensor(
-                out=windows[b % N_WIN][:].indirect(offsets[:, h * 32 : (h + 1) * 32]),
-                in0=dx[b][:, cols], in1=other, op=ALU.mult,
+                out=windows[b % N_WIN][:].indirect(offsets[:, j0 // 16 : j1 // 16]),
+                in0=dx[b][:, j0:j1], in1=other[:, j0:j1], op=ALU.mult,
             )
 
         def store(b):
             nc.sync.dma_start(out=out[b * P : (b + 1) * P, :], in_=windows[b % N_WIN][:])
 
-        top_w(0, "v")
-        hi_w(0)
-        lo_w(0)
-        cast_dy(0, 0)
-        quant_w(0)
-        quant_dy(0)
-        cast_dy(1, 128)
-        quant_dy(1)
-        top_w(1, "s")
-        matmul(0, 0)
-        hi_w(1)
-        lo_w(1)
-        nc.vector.tensor_tensor(out=blk(dx, 0, "dx")[:, 0:HALF], in0=acc[0, 0][:], in1=d_raw[0, 0][:], op=ALU.mult)
-        quant_w(1)
-        weigh_d(1, 0)
-        matmul(1, 0)
-        copy_dx(1, 0)
-        scatter_half(0, 0, wgo_a[:])
-        cast_dy(2, 0)
-        cast_dy(3, 0)
-        quant_dy(2)
-        quant_dy(3)
-        weigh_d(0, 1)
-        matmul(0, 1)
-        copy_dx(0, 1)
-        scatter_half(1, 0, dw[1][:, 0:HALF])
-        top_w(2, "s")
-        weigh_d(1, 1)
-        matmul(1, 1)
-        copy_dx(1, 1)
-        hi_w(2)
-        scatter_half(0, 1, dw[0][:, HALF:J])
-        store(0)
-
         def prepare(b):
             for h in range(2):
                 weigh_d(b, h)
                 matmul(b, h)
-                if b not in COPY_SCATTER:
-                    copy_dx(b, h)
+                copy_dx(b, h)
 
-        lo_w(2)
-        top_w(3, "s")
-        hi_w(3)
-        quant_w(2)
-        prepare(2)
-        scatter_half(1, 1, dw[1][:, HALF:J])
+        def prepare_half(b, h):
+            weigh_d(b, h)
+            matmul(b, h)
+            copy_dx(b, h)
+
+        turn_wgo()
+        top_w(0, 1, "v")
+        top_w(1, 1, "v")
+        hi_w(0, 1)
+        hi_w(1, 1)
+        lo_w(0, 1)
+        lo_w(1, 1)
+        cast_dy(0, 0)
+        quant_w(0, 1)
+        quant_w(1, 1)
+        quant_dy(0)
+        weigh_d(0, 0)
+        cast_dy(1, 256)
+        quant_dy(1)
+        matmul(0, 0)
+        copy_dx(0, 0)
+        prepare_half(1, 0)
+        top_w(2, 1, "v")
+        hi_w(2, 1)
+        lo_w(2, 1)
+        quant_w(2, 1)
+        scatter(0, 0, HALF, dw[0])
+        cast_dy(2, 0)
+        cast_dy(3, 0)
+        scatter(1, 0, 256, dw[1])
+        quant_dy(2)
+        quant_dy(3)
+        prepare_half(0, 1)
+        scatter(1, 256, HALF, dw[1])
+        top_w(3, 1, "v")
+        hi_w(3, 1)
+        lo_w(3, 1)
+        quant_w(3, 1)
+        prepare_half(1, 1)
+        scatter(0, HALF, J, dw[0])
+        store(0)
+        late_window(2, "dx0")
+        prepare_half(2, 0)
+        top_w(4, 2, "s")
+        scatter(1, HALF, J, dw[1])
         store(1)
-
-        for b in range(2, NB):
+        hi_w(4, 2)
+        prepare_half(2, 1)
+        top_w(6, 2, "s")
+        scatter(2, 0, HALF, dw[2])
+        lo_w(4, 2)
+        prepare(3)
+        scatter(2, HALF, J, dw[2])
+        store(2)
+        quant_w(4, 2)
+        hi_w(6, 2)
+        between = {3: [(lo_w, 6)], 4: [(quant_w, 6)]}
+        for b in range(3, NB):
             if b + 1 < NB:
-                lo_w(b + 1)
-                if b + 2 < NB:
-                    top_w(b + 2, "s")
-                    hi_w(b + 2)
-                quant_w(b + 1)
-            win = windows[b % N_WIN][:].indirect(offsets[:])
-            if b in COPY_SCATTER:
-                for h in range(2):
-                    cols = slice(h * HALF, (h + 1) * HALF)
-                    nc.vector.tensor_tensor(out=blk(dx, b, "dx")[:, cols], in0=acc[b, h][:], in1=dw[b][:, cols], op=ALU.mult)
-                if b + 1 < NB:
-                    prepare(b + 1)
-                nc.vector.tensor_copy(out=win, in_=dx[b][:])
-            else:
-                if b + 1 < NB:
-                    prepare(b + 1)
-                nc.vector.tensor_tensor(out=win, in0=dx[b][:], in1=dw[b][:], op=ALU.mult)
+                prepare(b + 1)
+            scatter(b, 0, J, dw[b])
             store(b)
+            for step, unit in between.get(b, []):
+                step(unit, 2)

@@ -36,7 +36,6 @@ def tile_list_embg_hl_mul_kernel(tc, dy, w, d, wgo, offs, out):
         t2_ps = ctx.enter_context(tc.psum_pool(name="t2_ps", bufs=2))
 
         offsets = lists.tile([P, J // 16], U16, name="offsets")
-        nc.sync.dma_start(offsets[:], offs)
 
         w4 = w.rearrange("(p t) n -> p t n", t=PACK)
         dy4 = dy.rearrange("(p t) j -> p t j", t=PACK)
@@ -52,7 +51,7 @@ def tile_list_embg_hl_mul_kernel(tc, dy, w, d, wgo, offs, out):
         nc.scalar.activation(out=ident[:], in_=ident0[:], func=COPY)
 
         windows = {}
-        for i in range(2):
+        for i in range(1):
             windows[i] = keep.tile([P, T], F32, name=f"win{i}")
             nc.vector.memset(windows[i][:], 0.0)
 
@@ -74,22 +73,21 @@ def tile_list_embg_hl_mul_kernel(tc, dy, w, d, wgo, offs, out):
 
         w_unit[0] = load("w0", [P, PACK, P], w4[:, :, 0:P])
         w_unit[1] = load("w1", [P, PACK, P], w4[:, :, P : 2 * P])
-        stage = load("stage", [P, P], wgo.rearrange("r (c p) -> (r c) p", p=P)[0:P, :])
-        dy_raw[0] = load("dy0", [P, PACK, 256], dy4[:, :, 0:256])
-        d_raw[0, 0] = load("d00", [P, HALF], d[0:P, 0:HALF])
-        dy_raw[1] = load("dy1", [P, PACK, 256], dy4[:, :, 256:512])
         load_w_pair(2)
-        w_unit[3] = w_unit[2][:, :, P : 2 * P]
-        w_unit[2] = w_unit[2][:, :, 0:P]
+        dy_raw[0] = load("dy0", [P, PACK, 256], dy4[:, :, 0:256])
+        dy_raw[1] = load("dy1", [P, PACK, 256], dy4[:, :, 256:512])
+        load_w_pair(4)
+        d_raw[0, 0] = load("d00", [P, HALF], d[0:P, 0:HALF])
+        wgo_a = load("wgo_a", [P, HALF], wgo[:, 0:HALF])
+        nc.sync.dma_start(offsets[:], offs)
+        stage = load("stage", [P, P], wgo.rearrange("r (c p) -> (r c) p", p=P)[0:P, :])
         d_raw[1, 0] = load("d10", [P, HALF], d[P : 2 * P, 0:HALF])
         dy_raw[2] = load("dy2", [P, PACK, 256], dy4[:, :, 512:768])
         dy_raw[3] = load("dy3", [P, PACK, 256], dy4[:, :, 768:1024])
         d_raw[0, 1] = load("d01", [P, HALF], d[0:P, HALF:J])
-        d_raw[1, 1] = load("d11", [P, HALF], d[P : 2 * P, HALF:J])
-        load_d(2)
-        load_w_pair(4)
         load_w_pair(6)
-        for b in range(3, NB):
+        d_raw[1, 1] = load("d11", [P, HALF], d[P : 2 * P, HALF:J])
+        for b in range(2, NB):
             load_d(b)
 
         wgo_t = keep.tile([P, 8], F32, name="wgo_t")
@@ -110,14 +108,11 @@ def tile_list_embg_hl_mul_kernel(tc, dy, w, d, wgo, offs, out):
 
         dy_bf = {}
 
-        def cast_dy(q, vec_cols):
+        def cast_dy(q):
             tl = keep.tile([P, 256 * PACK], BF16, name=f"dybf{q}", tag=f"dybf{q}", align_bytes=64)
             dy_bf[q] = tl
-            s = 256 - vec_cols
-            if s:
-                nc.scalar.copy(out=il(tl[:, 0 : s * PACK]), in_=pl(dy_raw[q][:, :, 0:s]))
-            if vec_cols:
-                nc.vector.tensor_copy(out=il(tl[:, s * PACK :]), in_=pl(dy_raw[q][:, :, s:256]))
+            for s in range(0, 256, 128):
+                nc.scalar.copy(out=il(tl[:, s * PACK : (s + 128) * PACK]), in_=pl(dy_raw[q][:, :, s : s + 128]))
 
         def quant_dy(q):
             cols = slice(q * 256, (q + 1) * 256)
@@ -223,58 +218,55 @@ def tile_list_embg_hl_mul_kernel(tc, dy, w, d, wgo, offs, out):
             matmul(b, h)
             copy_dx(b, h)
 
-        turn_wgo()
         top_w(0, 1, "v")
-        top_w(1, 1, "v")
+        top_w(1, 1, "s")
+        top_w(2, 2, "s")
         hi_w(0, 1)
-        hi_w(1, 1)
         lo_w(0, 1)
-        lo_w(1, 1)
-        cast_dy(0, 0)
+        hi_w(1, 1)
         quant_w(0, 1)
-        quant_w(1, 1)
+        lo_w(1, 1)
+        cast_dy(0)
+        cast_dy(1)
         quant_dy(0)
-        weigh_d(0, 0)
-        cast_dy(1, 256)
         quant_dy(1)
+        hi_w(2, 2)
+        quant_w(1, 1)
+        lo_w(2, 2)
         matmul(0, 0)
-        copy_dx(0, 0)
+        nc.vector.tensor_tensor(out=dx[0][:, 0:HALF], in0=acc[0, 0][:], in1=d_raw[0, 0][:], op=ALU.mult)
+        quant_w(2, 2)
+        top_w(4, 2, "v")
+        hi_w(4, 2)
+        lo_w(4, 2)
+        late_window(1, "w4")
+        turn_wgo()
         prepare_half(1, 0)
-        top_w(2, 1, "v")
-        hi_w(2, 1)
-        lo_w(2, 1)
-        quant_w(2, 1)
-        scatter(0, 0, HALF, dw[0])
-        cast_dy(2, 0)
-        cast_dy(3, 0)
+        scatter(0, 0, HALF, wgo_a)
+        quant_w(4, 2)
+        cast_dy(2)
+        cast_dy(3)
         scatter(1, 0, 256, dw[1])
         quant_dy(2)
         quant_dy(3)
         prepare_half(0, 1)
         scatter(1, 256, HALF, dw[1])
-        top_w(3, 1, "v")
-        hi_w(3, 1)
-        lo_w(3, 1)
-        quant_w(3, 1)
         prepare_half(1, 1)
         scatter(0, HALF, J, dw[0])
         store(0)
         late_window(2, "dx0")
         prepare_half(2, 0)
-        top_w(4, 2, "s")
         scatter(1, HALF, J, dw[1])
         store(1)
-        hi_w(4, 2)
         prepare_half(2, 1)
         top_w(6, 2, "s")
         scatter(2, 0, HALF, dw[2])
-        lo_w(4, 2)
+        hi_w(6, 2)
         prepare(3)
         scatter(2, HALF, J, dw[2])
         store(2)
-        quant_w(4, 2)
-        hi_w(6, 2)
-        between = {3: [(lo_w, 6)], 4: [(quant_w, 6)]}
+        lo_w(6, 2)
+        between = {3: [(quant_w, 6)]}
         for b in range(3, NB):
             if b + 1 < NB:
                 prepare(b + 1)

@@ -22,6 +22,8 @@ PACK = 4
 HALF = 512
 NB = N // P
 HI_MASK = -983056
+HI_MASK32 = -1048576
+SIGN32 = -2147483648
 N_WIN = 3
 
 
@@ -36,6 +38,7 @@ def tile_list_embg_hl_mul_kernel(tc, dy, w, d, wgo, offs, out):
         t2_ps = ctx.enter_context(tc.psum_pool(name="t2_ps", bufs=2))
 
         offsets = lists.tile([P, J // 16], U16, name="offsets")
+        nc.sync.dma_start(offsets[:], offs)
 
         w4 = w.rearrange("(p t) n -> p t n", t=PACK)
         dy4 = dy.rearrange("(p t) j -> p t j", t=PACK)
@@ -79,11 +82,10 @@ def tile_list_embg_hl_mul_kernel(tc, dy, w, d, wgo, offs, out):
         load_w_pair(4)
         d_raw[0, 0] = load("d00", [P, HALF], d[0:P, 0:HALF])
         wgo_a = load("wgo_a", [P, HALF], wgo[:, 0:HALF])
-        nc.sync.dma_start(offsets[:], offs)
         stage = load("stage", [P, P], wgo.rearrange("r (c p) -> (r c) p", p=P)[0:P, :])
-        d_raw[1, 0] = load("d10", [P, HALF], d[P : 2 * P, 0:HALF])
         dy_raw[2] = load("dy2", [P, PACK, 256], dy4[:, :, 512:768])
         dy_raw[3] = load("dy3", [P, PACK, 256], dy4[:, :, 768:1024])
+        d_raw[1, 0] = load("d10", [P, HALF], d[P : 2 * P, 0:HALF])
         d_raw[0, 1] = load("d01", [P, HALF], d[0:P, HALF:J])
         load_w_pair(6)
         d_raw[1, 1] = load("d11", [P, HALF], d[P : 2 * P, HALF:J])
@@ -158,6 +160,42 @@ def tile_list_embg_hl_mul_kernel(tc, dy, w, d, wgo, offs, out):
                     cols = slice((part * nb + i) * P, (part * nb + i + 1) * P)
                     w_codes[b + i, part] = codes[:, cols]
                     w_scales[b + i, part] = scales[:, cols]
+
+        neg_hi = {}
+
+        def neg_hi_w(b, nb):
+            tl = keep.tile([P, PACK, nb * P], F32, name=f"nh{b}")
+            neg_hi[b] = tl
+            nc.vector.tensor_scalar(
+                out=tl[:].bitcast(I32), in0=w_unit[b][:].bitcast(I32),
+                scalar1=HI_MASK32, scalar2=SIGN32, op0=ALU.bitwise_and, op1=ALU.bitwise_xor,
+            )
+
+        def split_on_tensor(b, nb):
+            width = nb * P * PACK
+            tl = keep.tile([P, 2 * width], BF16, name=f"hl{b}", tag=f"hl{b}", align_bytes=64)
+            hl[b] = tl
+            nc.scalar.activation(out=il(tl[:, 0:width]), in_=pl(neg_hi[b][:]), func=COPY, scale=-1.0)
+            back = t2_ps.tile([P, HALF], F32, name="t2")
+            for i in range(nb):
+                cols = slice(i * P, (i + 1) * P)
+                turned = t1_ps.tile([P, HALF], F32, name="t1")
+                for t in range(PACK):
+                    dst = turned[:, t * P : (t + 1) * P]
+                    nc.tensor.matmul(dst, w_unit[b][:, t, cols], ident[:], start=True, stop=False, is_transpose=True)
+                    nc.tensor.matmul(dst, neg_hi[b][:, t, cols], ident[:], start=False, stop=True, is_transpose=True)
+                lo_t = ring.tile([P, P * PACK], BF16, name="lo_t")
+                nc.scalar.copy(
+                    out=lo_t[:].rearrange("n (u p e) -> n u p e", u=2, e=2),
+                    in_=turned[:].rearrange("n (u e p) -> n u p e", u=2, e=2),
+                )
+                words = lo_t[:].bitcast(F32)
+                for u in range(2):
+                    nc.tensor.transpose(back[:, (2 * i + u) * P : (2 * i + u + 1) * P], words[:, u * P : (u + 1) * P], ident[:])
+            nc.scalar.copy(
+                out=tl[:, width:].bitcast(F32).rearrange("p (i n u) -> p i n u", i=nb, u=2),
+                in_=back[:].rearrange("p (i u n) -> p i n u", i=nb, u=2),
+            )
 
         acc = {}
 
@@ -241,16 +279,15 @@ def tile_list_embg_hl_mul_kernel(tc, dy, w, d, wgo, offs, out):
         lo_w(4, 2)
         late_window(1, "w4")
         turn_wgo()
+        cast_dy(2)
+        cast_dy(3)
         prepare_half(1, 0)
         scatter(0, 0, HALF, wgo_a)
         quant_w(4, 2)
-        cast_dy(2)
-        cast_dy(3)
-        scatter(1, 0, 256, dw[1])
         quant_dy(2)
         quant_dy(3)
         prepare_half(0, 1)
-        scatter(1, 256, HALF, dw[1])
+        scatter(1, 0, HALF, dw[1])
         prepare_half(1, 1)
         scatter(0, HALF, J, dw[0])
         store(0)
@@ -258,19 +295,17 @@ def tile_list_embg_hl_mul_kernel(tc, dy, w, d, wgo, offs, out):
         prepare_half(2, 0)
         scatter(1, HALF, J, dw[1])
         store(1)
+        neg_hi_w(6, 2)
         prepare_half(2, 1)
-        top_w(6, 2, "s")
         scatter(2, 0, HALF, dw[2])
-        hi_w(6, 2)
         prepare(3)
         scatter(2, HALF, J, dw[2])
         store(2)
-        lo_w(6, 2)
-        between = {3: [(quant_w, 6)]}
+        split_on_tensor(6, 2)
         for b in range(3, NB):
             if b + 1 < NB:
                 prepare(b + 1)
             scatter(b, 0, J, dw[b])
             store(b)
-            for step, unit in between.get(b, []):
-                step(unit, 2)
+            if b == 4:
+                quant_w(6, 2)

from contextlib import ExitStack

import concourse.mybir as mybir
from concourse.masks import make_identity

K, N, T, J = 512, 1024, 2048, 1024
FLOPS = 2 * 2 * K * N * J

F32 = mybir.dt.float32
BF16 = mybir.dt.bfloat16
I32 = mybir.dt.int32
U32 = mybir.dt.uint32
U16 = mybir.dt.uint16
U8 = mybir.dt.uint8
E4M3 = mybir.dt.float8_e4m3fn_x4
E5M2 = mybir.dt.float8_e5m2_x4
ALU = mybir.AluOpType
COPY = mybir.ActivationFunctionType.Copy

P = 128
PACK = 4
HALF = 512
NB = N // P
HI_MASK = -983056
HI_MASK32 = -1048576
SIGN32 = -2147483648
N_WIN = 3


def tile_list_embg_hl_mul_kernel(tc, dy, w, d, wgo, offs, out):
    nc = tc.nc
    with ExitStack() as ctx:
        lists = ctx.enter_context(tc.tile_pool(name="lists", bufs=1))
        keep = ctx.enter_context(tc.tile_pool(name="keep", bufs=1))
        ring = ctx.enter_context(tc.tile_pool(name="ring", bufs=4))
        mm_ps = ctx.enter_context(tc.psum_pool(name="mm_ps", bufs=4))
        t1_ps = ctx.enter_context(tc.psum_pool(name="t1_ps", bufs=2))
        t2_ps = ctx.enter_context(tc.psum_pool(name="t2_ps", bufs=2))

        offsets = lists.tile([P, J // 16], U16, name="offsets")
        nc.sync.dma_start(offsets[:], offs)

        w4 = w.rearrange("(p t) n -> p t n", t=PACK)
        dy4 = dy.rearrange("(p t) j -> p t j", t=PACK)

        def load(name, shape, src):
            tl = keep.tile(shape, F32, name=name, tag=name, align_bytes=64)
            nc.sync.dma_start(out=tl[:], in_=src)
            return tl

        ident0 = keep.tile([P, P], F32, name="ident0")
        make_identity(nc, ident0[:])
        ident = keep.tile([P, P], F32, name="ident")
        nc.scalar.activation(out=ident[:], in_=ident0[:], func=COPY)

        windows = {}
        for i in range(1):
            windows[i] = keep.tile([P, T], F32, name=f"win{i}")
            nc.vector.memset(windows[i][:], 0.0)

        def late_window(i, tag):
            windows[i] = keep.tile([P, T], F32, name=f"win{i}", tag=tag, align_bytes=64)
            nc.gpsimd.memset(windows[i][:], 0.0)

        w_unit = {}
        dy_raw = {}
        d_raw = {}
        def load_w_pair(b):
            pair = load(f"w{b}", [P, PACK, 2 * P], w4[:, :, b * P : (b + 2) * P])
            w_unit[b] = pair

        def load_d(b):
            whole = load(f"d{b}", [P, J], d[b * P : (b + 1) * P, :])
            d_raw[b, 0] = whole[:, 0:HALF]
            d_raw[b, 1] = whole[:, HALF:J]

        w_unit[0] = load("w0", [P, PACK, P], w4[:, :, 0:P])
        w_unit[1] = load("w1", [P, PACK, P], w4[:, :, P : 2 * P])
        load_w_pair(2)
        dy_raw[0] = load("dy0", [P, PACK, 256], dy4[:, :, 0:256])
        dy_raw[1] = load("dy1", [P, PACK, 256], dy4[:, :, 256:512])
        load_w_pair(4)
        d_raw[0, 0] = load("d00", [P, HALF], d[0:P, 0:HALF])
        wgo_a = load("wgo_a", [P, HALF], wgo[:, 0:HALF])
        stage = load("stage", [P, P], wgo.rearrange("r (c p) -> (r c) p", p=P)[0:P, :])
        dy_raw[2] = load("dy2", [P, PACK, 256], dy4[:, :, 512:768])
        dy_raw[3] = load("dy3", [P, PACK, 256], dy4[:, :, 768:1024])
        d_raw[1, 0] = load("d10", [P, HALF], d[P : 2 * P, 0:HALF])
        d_raw[0, 1] = load("d01", [P, HALF], d[0:P, HALF:J])
        load_w_pair(6)
        d_raw[1, 1] = load("d11", [P, HALF], d[P : 2 * P, HALF:J])
        for b in range(2, NB):
            load_d(b)

        wgo_t = keep.tile([P, 8], F32, name="wgo_t")

        def turn_wgo():
            wgo_ps = t1_ps.tile([P, HALF], F32, name="t1")
            nc.tensor.transpose(wgo_ps[:, 0:P], stage[:], ident[:])
            nc.scalar.copy(out=wgo_t[:], in_=wgo_ps[:, 0:8])

        dy_codes = keep.tile([P, J], U32, name="dy_codes", align_bytes=64)
        dy_scales = keep.tile([P, J], U8, name="dy_scales", align_bytes=64)

        def il(ap):
            return ap.rearrange("p (c i t) -> p c t i", i=2, t=PACK)

        def pl(ap):
            return ap.rearrange("p t (c i) -> p c t i", i=2)

        dy_bf = {}

        def cast_dy(q):
            tl = keep.tile([P, 256 * PACK], BF16, name=f"dybf{q}", tag=f"dybf{q}", align_bytes=64)
            dy_bf[q] = tl
            for s in range(0, 256, 128):
                nc.scalar.copy(out=il(tl[:, s * PACK : (s + 128) * PACK]), in_=pl(dy_raw[q][:, :, s : s + 128]))

        def quant_dy(q):
            cols = slice(q * 256, (q + 1) * 256)
            nc.vector.quantize_mx(out=dy_codes[:, cols].bitcast(E5M2), scales=dy_scales[:, cols], in_=dy_bf[q][:])

        top = {}
        hl = {}
        w_codes = {}
        w_scales = {}

        def top_w(b, nb, eng):
            width = nb * P * PACK
            tl = ring.tile([P, width], BF16, name="top", align_bytes=64)
            top[b] = tl
            src = pl(w_unit[b][:, :, :].bitcast(BF16)[:, :, 1::2])
            if eng == "v":
                nc.vector.tensor_copy(out=il(tl[:]), in_=src)
            else:
                nc.scalar.copy(out=il(tl[:]), in_=src)

        def hi_w(b, nb):
            width = nb * P * PACK
            tl = keep.tile([P, 2 * width], BF16, name=f"hl{b}", tag=f"hl{b}", align_bytes=64)
            hl[b] = tl
            nc.vector.tensor_scalar(
                out=tl[:, 0:width].bitcast(I32), in0=top[b][:].bitcast(I32),
                scalar1=HI_MASK, scalar2=None, op0=ALU.bitwise_and,
            )

        def lo_w(b, nb):
            width = nb * P * PACK
            tl = hl[b]
            nc.vector.tensor_tensor(
                out=il(tl[:, width:]), in0=pl(w_unit[b][:, :, :]), in1=il(tl[:, 0:width]), op=ALU.subtract
            )

        def quant_w(b, nb):
            codes = keep.tile([P, 2 * nb * P], U32, name=f"wc{b}", align_bytes=64)
            scales = keep.tile([P, 2 * nb * P], U8, name=f"ws{b}", align_bytes=64)
            nc.vector.quantize_mx(out=codes[:].bitcast(E4M3), scales=scales[:], in_=hl[b][:])
            for i in range(nb):
                for part in range(2):
                    cols = slice((part * nb + i) * P, (part * nb + i + 1) * P)
                    w_codes[b + i, part] = codes[:, cols]
                    w_scales[b + i, part] = scales[:, cols]

        neg_hi = {}

        def neg_hi_w(b, nb):
            tl = keep.tile([P, PACK, nb * P], F32, name=f"nh{b}")
            neg_hi[b] = tl
            nc.vector.tensor_scalar(
                out=tl[:].bitcast(I32), in0=w_unit[b][:].bitcast(I32),
                scalar1=HI_MASK32, scalar2=SIGN32, op0=ALU.bitwise_and, op1=ALU.bitwise_xor,
            )

        def split_on_tensor(b, nb):
            width = nb * P * PACK
            tl = keep.tile([P, 2 * width], BF16, name=f"hl{b}", tag=f"hl{b}", align_bytes=64)
            hl[b] = tl
            nc.scalar.activation(out=il(tl[:, 0:width]), in_=pl(neg_hi[b][:]), func=COPY, scale=-1.0)
            back = t2_ps.tile([P, HALF], F32, name="t2")
            for i in range(nb):
                cols = slice(i * P, (i + 1) * P)
                turned = t1_ps.tile([P, HALF], F32, name="t1")
                for t in range(PACK):
                    dst = turned[:, t * P : (t + 1) * P]
                    nc.tensor.matmul(dst, w_unit[b][:, t, cols], ident[:], start=True, stop=False, is_transpose=True)
                    nc.tensor.matmul(dst, neg_hi[b][:, t, cols], ident[:], start=False, stop=True, is_transpose=True)
                lo_t = ring.tile([P, P * PACK], BF16, name="lo_t")
                nc.scalar.copy(
                    out=lo_t[:].rearrange("n (u p e) -> n u p e", u=2, e=2),
                    in_=turned[:].rearrange("n (u e p) -> n u p e", u=2, e=2),
                )
                words = lo_t[:].bitcast(F32)
                for u in range(2):
                    nc.tensor.transpose(back[:, (2 * i + u) * P : (2 * i + u + 1) * P], words[:, u * P : (u + 1) * P], ident[:])
            nc.scalar.copy(
                out=tl[:, width:].bitcast(F32).rearrange("p (i n u) -> p i n u", i=nb, u=2),
                in_=back[:].rearrange("p (i u n) -> p i n u", i=nb, u=2),
            )

        acc = {}

        def matmul(b, h):
            ps = mm_ps.tile([P, HALF], F32, name="mm")
            acc[b, h] = ps
            cols = slice(h * HALF, (h + 1) * HALF)
            for part in range(2):
                nc.tensor.matmul_mx(
                    out=ps[:], lhsT=w_codes[b, part].bitcast(E4M3), lhsT_scale=w_scales[b, part],
                    rhs=dy_codes[:, cols].bitcast(E5M2), rhs_scale=dy_scales[:, cols],
                    start=(part == 0), stop=(part == 1),
                )

        dx = {0: keep.tile([P, J], F32, name="dx0", tag="dx0", align_bytes=64)}
        dw = {}

        def blk(store, b, name):
            if b not in store:
                store[b] = ring.tile([P, J], F32, name=name)
            return store[b]

        def weigh_d(b, h):
            t1 = t1_ps.tile([P, HALF], F32, name="t1")
            for c in range(4):
                nc.tensor.transpose(t1[:, c * P : (c + 1) * P], d_raw[b, h][:, c * P : (c + 1) * P], ident[:])
            dt = ring.tile([P, HALF], F32, name="dt")
            for c in range(4):
                nc.scalar.activation(
                    out=dt[:, c * P : (c + 1) * P], in_=t1[:, c * P : (c + 1) * P], func=COPY,
                    scale=wgo_t[:, 4 * h + c : 4 * h + c + 1],
                )
            t2 = t2_ps.tile([P, HALF], F32, name="t2")
            for c in range(4):
                nc.tensor.transpose(t2[:, c * P : (c + 1) * P], dt[:, c * P : (c + 1) * P], ident[:])
            nc.scalar.copy(out=blk(dw, b, "dw")[:, h * HALF : (h + 1) * HALF], in_=t2[:])

        def copy_dx(b, h):
            nc.scalar.copy(out=blk(dx, b, "dx")[:, h * HALF : (h + 1) * HALF], in_=acc[b, h][:])

        def scatter(b, j0, j1, other):
            nc.vector.tensor_tensor(
                out=windows[b % N_WIN][:].indirect(offsets[:, j0 // 16 : j1 // 16]),
                in0=dx[b][:, j0:j1], in1=other[:, j0:j1], op=ALU.mult,
            )

        def store(b):
            nc.sync.dma_start(out=out[b * P : (b + 1) * P, :], in_=windows[b % N_WIN][:])

        def prepare(b):
            for h in range(2):
                weigh_d(b, h)
                matmul(b, h)
                copy_dx(b, h)

        def prepare_half(b, h):
            weigh_d(b, h)
            matmul(b, h)
            copy_dx(b, h)

        top_w(0, 1, "v")
        top_w(1, 1, "s")
        top_w(2, 2, "s")
        hi_w(0, 1)
        lo_w(0, 1)
        hi_w(1, 1)
        quant_w(0, 1)
        lo_w(1, 1)
        cast_dy(0)
        cast_dy(1)
        quant_dy(0)
        quant_dy(1)
        hi_w(2, 2)
        quant_w(1, 1)
        lo_w(2, 2)
        matmul(0, 0)
        nc.vector.tensor_tensor(out=dx[0][:, 0:HALF], in0=acc[0, 0][:], in1=d_raw[0, 0][:], op=ALU.mult)
        quant_w(2, 2)
        top_w(4, 2, "v")
        hi_w(4, 2)
        lo_w(4, 2)
        late_window(1, "w4")
        turn_wgo()
        cast_dy(2)
        cast_dy(3)
        prepare_half(1, 0)
        scatter(0, 0, HALF, wgo_a)
        quant_w(4, 2)
        quant_dy(2)
        quant_dy(3)
        prepare_half(0, 1)
        scatter(1, 0, HALF, dw[1])
        prepare_half(1, 1)
        scatter(0, HALF, J, dw[0])
        store(0)
        late_window(2, "dx0")
        prepare_half(2, 0)
        scatter(1, HALF, J, dw[1])
        store(1)
        neg_hi_w(6, 2)
        prepare_half(2, 1)
        scatter(2, 0, HALF, dw[2])
        prepare(3)
        scatter(2, HALF, J, dw[2])
        store(2)
        split_on_tensor(6, 2)
        for b in range(3, NB):
            if b + 1 < NB:
                prepare(b + 1)
            scatter(b, 0, J, dw[b])
            store(b)
            if b == 4:
                quant_w(6, 2)
